import numpy as np, ml_dtypes
CORES = [112,113,114,115,124,125,126,127]
N = 8
WIDTHS = [2048,1024,512,1024,1024,2048,2048,2048]
XW = 2048
def setup_inputs(rng):
    return {"x": rng.standard_normal((N, 128, XW), dtype=np.float32).astype(ml_dtypes.bfloat16)}
def reference(x):
    g = np.concatenate([x[r][:, :WIDTHS[r]] for r in range(N)], axis=1)
    return {"y": np.broadcast_to(g, (N,) + g.shape)}

@@ -1,0 +1,115 @@
+from concourse.bass import DstId, RemoteDMATransfer
+
+SCRATCH = {
+    "gat": ("sbuf", [128, 11776], "bfloat16"),
+}
+SEMAPHORES = ["ld", "hp", "xc", "snt", "st_s", "st_a",
+              "ag0", "ag1", "ag2", "ag3", "fo0", "fo1", "fo2", "fo3"]
+
+
+def plan(T, topo):
+    widths = T.tables["WIDTHS"]
+    cores = list(T.cores)
+    off = [0]
+    for w in widths:
+        off.append(off[-1] + w)
+    chips = sorted(set(topo.chip(c) for c in cores))
+    members = {ch: [r for r, c in enumerate(cores) if topo.chip(c) == ch] for ch in chips}
+    quarters = {}
+    for ch in chips:
+        other = [o for o in chips if o != ch][0]
+        probe = cores[members[other][0]]
+        gates = [c for c in range(ch * 8, ch * 8 + 8) if topo.may_write(c, probe)]
+        lo = off[members[ch][0]]
+        hi = off[members[ch][-1] + 1]
+        q = (hi - lo) // 4
+        helpers = [c for c in gates if c not in cores]
+        inside = [c for c in gates if c in cores]
+        order = helpers + inside
+        quarters[ch] = [(order[k], lo + k * q, lo + (k + 1) * q) for k in range(4)]
+    return widths, cores, off, chips, members, quarters
+
+
+def rank_program(g, core, T, topo):
+    widths, cores, off, chips, members, quarters = plan(T, topo)
+    ch = topo.chip(core)
+    if ch not in chips:
+        return
+    other = [o for o in chips if o != ch][0]
+    rank = T.rank_of(core)
+    gat = T.gat
+    sem = T.sem
+    sent = [0]
+
+    def one(dst, lo, hi, rsem):
+        rid, pid, _se = topo.addr(dst)
+        m = topo.mask(core, dst)
+        g.remote_dma(gat[:, lo:hi], gat[:, lo:hi], rsem, sem.snt, pid, rid, m)
+        sent[0] += bin(m).count("1")
+
+    def many(dsts, lo, hi, rsem):
+        ids = []
+        for d in dsts:
+            rid, pid, _se = topo.addr(d)
+            ids.append(DstId(rid=rid, pnc=pid))
+        g.remote_dma_fused([RemoteDMATransfer(dst_ids=ids, dma_engine_mask=0xFFFF, remote_sem=rsem,
+                                              srcs=[gat[:, lo:hi]], dsts=[gat[:, lo:hi] for _d in dsts], alu_op=0)],
+                           local_sem=sem.snt)
+        sent[0] += 16
+
+    mine = [k for k, (gc, lo, hi) in enumerate(quarters[ch]) if gc == core]
+
+    if rank is None:
+        if not mine:
+            return
+        k = mine[0]
+        _gc, lo, hi = quarters[ch][k]
+        n = sum(1 for r in members[ch] if max(lo, off[r]) < min(hi, off[r + 1]))
+        g.wait_ge(sem.hp, 16 * n)
+        one(cores[members[other][k]], lo, hi, sem.xc)
+        g.wait_ge(sem.snt, sent[0])
+        return
+
+    w = widths[rank]
+    a, b = off[rank], off[rank + 1]
+    idx = members[ch].index(rank)
+    peers = [cores[r] for r in members[ch] if r != rank]
+
+    g.sync.dma_start(gat[:, a:b], T.x[:, 0:w]).then_inc(sem.ld, 16)
+    g.scalar.dma_start(T.y[:, a:b], T.x[:, 0:w]).then_inc(sem.st_a, 16)
+    n_a = 1
+    n_s = 0
+    g.wait_ge(sem.ld, 16)
+
+    for gc, lo, hi in quarters[ch]:
+        if gc not in cores and max(lo, a) < min(hi, b):
+            one(gc, max(lo, a), min(hi, b), sem.hp)
+    many(peers, a, b, sem["ag%d" % idx])
+    if mine:
+        k = mine[0]
+        _gc, lo, hi = quarters[ch][k]
+        for j, r in enumerate(members[ch]):
+            if r != rank and max(lo, off[r]) < min(hi, off[r + 1]):
+                g.wait_ge(sem["ag%d" % j], 16)
+        one(cores[members[other][k]], lo, hi, sem.xc)
+    _gc, qlo, qhi = quarters[other][idx]
+    g.wait_ge(sem.xc, 8)
+    many(peers, qlo, qhi, sem["fo%d" % idx])
+
+    for j, r in enumerate(members[ch]):
+        if r != rank:
+            g.sync.wait_ge(sem["ag%d" % j], 16)
+            g.sync.dma_start(T.y[:, off[r]:off[r + 1]], gat[:, off[r]:off[r + 1]]).then_inc(sem.st_s, 16)
+            n_s += 1
+    g.scalar.wait_ge(sem.xc, 8)
+    g.scalar.dma_start(T.y[:, qlo:qhi], gat[:, qlo:qhi]).then_inc(sem.st_a, 16)
+    n_a += 1
+    for j in range(4):
+        if j != idx:
+            _gc, lo, hi = quarters[other][j]
+            g.scalar.wait_ge(sem["fo%d" % j], 16)
+            g.scalar.dma_start(T.y[:, lo:hi], gat[:, lo:hi]).then_inc(sem.st_a, 16)
+            n_a += 1
+    g.sync.wait_ge(sem.st_s, 16 * n_s)
+    g.scalar.wait_ge(sem.st_a, 16 * n_a)
+    g.wait_ge(sem.snt, sent[0])

@@ -3,113 +3,177 @@ from concourse.bass import DstId, RemoteDMATransfer
 SCRATCH = {
     "gat": ("sbuf", [128, 11776], "bfloat16"),
 }
-SEMAPHORES = ["ld", "hp", "xc", "snt", "st_s", "st_a",
-              "ag0", "ag1", "ag2", "ag3", "fo0", "fo1", "fo2", "fo3"]
+SEMAPHORES = (["ld", "fs", "snt", "st_s", "st_a", "fd0", "fd1", "xc0", "xc1"]
+              + ["ag%d" % i for i in range(8)] + ["in%d" % i for i in range(8)])
+
+LOW, HIGH, ALL = 0x00FF, 0xFF00, 0xFFFF
 
 
-def plan(T, topo):
-    widths = T.tables["WIDTHS"]
-    cores = list(T.cores)
+def perms(items):
+    if len(items) <= 1:
+        return [list(items)]
+    out = []
+    for i in range(len(items)):
+        for rest in perms(items[:i] + items[i + 1:]):
+            out.append([items[i]] + rest)
+    return out
+
+
+def plan(widths, cores, topo):
     off = [0]
     for w in widths:
         off.append(off[-1] + w)
     chips = sorted(set(topo.chip(c) for c in cores))
-    members = {ch: [r for r, c in enumerate(cores) if topo.chip(c) == ch] for ch in chips}
-    quarters = {}
+    tab = {}
     for ch in chips:
         other = [o for o in chips if o != ch][0]
-        probe = cores[members[other][0]]
-        gates = [c for c in range(ch * 8, ch * 8 + 8) if topo.may_write(c, probe)]
-        lo = off[members[ch][0]]
-        hi = off[members[ch][-1] + 1]
-        q = (hi - lo) // 4
-        helpers = [c for c in gates if c not in cores]
-        inside = [c for c in gates if c in cores]
-        order = helpers + inside
-        quarters[ch] = [(order[k], lo + k * q, lo + (k + 1) * q) for k in range(4)]
-    return widths, cores, off, chips, members, quarters
+        mem = [r for r, c in enumerate(cores) if topo.chip(c) == ch]
+        probe = [c for c in cores if topo.chip(c) == other][0]
+        allc = list(range(ch * 8, ch * 8 + 8))
+        gates = [c for c in allc if topo.may_write(c, probe)]
+        hg = [c for c in gates if c not in cores]
+        rg = [c for c in gates if c in cores]
+        free = [c for c in allc if c not in cores and c not in gates]
+        lo, hi = off[mem[0]], off[mem[-1] + 1]
+        mid = (lo + hi) // 2
+        cuts = [lo, (lo + mid) // 2, mid, off[cores.index(rg[1])], hi]
+        pieces = []
+        for k, gc in enumerate(hg + rg):
+            part = []
+            for r in mem:
+                s, e = max(cuts[k], off[r]), min(cuts[k + 1], off[r + 1])
+                if s < e:
+                    part.append((s, e, r))
+            if len(part) == 1:
+                s, e, r = part[0]
+                part = [(s, (s + e) // 2, r), ((s + e) // 2, e, r)]
+            part.sort(key=lambda t: (cores[t[2]] != gc, t[0]))
+            for slot, (s, e, r) in enumerate(part):
+                pieces.append({"lo": s, "hi": e, "owner": r, "gate": gc, "slot": slot,
+                               "dist": gc if gc in hg else free[k - 2]})
+        pieces.sort(key=lambda p: p["lo"])
+        for i, p in enumerate(pieces):
+            p["idx"] = i
+            p["to"] = [cores[r] for r in mem if r != p["owner"] and cores[r] != p["gate"]]
+            p["fd_n"] = 8 if cores[p["owner"]] in rg else 16
+            p["ag_n"] = 8 if p["dist"] in hg else 16
+        tab[ch] = {"mem": mem, "hg": hg, "rg": rg, "free": free, "pieces": pieces, "other": other}
+    for ch in chips:
+        helpers = tab[ch]["hg"] + tab[ch]["free"]
+        base = {h: 0 for h in helpers}
+        for p in tab[ch]["pieces"]:
+            n = p["hi"] - p["lo"]
+            base[p["dist"]] += n * len(p["to"]) + (n if p["gate"] == p["dist"] else 0)
+        inc = tab[tab[ch]["other"]]["pieces"]
+        by_slot = [[p for p in inc if p["slot"] == s] for s in (0, 1)]
+        best = None
+        for a in perms(helpers):
+            for b in perms(helpers):
+                load = dict(base)
+                for ps, hs in ((by_slot[0], a), (by_slot[1], b)):
+                    for p, h in zip(ps, hs):
+                        load[h] += 4 * (p["hi"] - p["lo"])
+                m = max(load.values())
+                if best is None or m < best[0]:
+                    best = (m, a, b)
+        for ps, hs in ((by_slot[0], best[1]), (by_slot[1], best[2])):
+            for p, h in zip(ps, hs):
+                p["land"] = h
+    return off, tab
 
 
 def rank_program(g, core, T, topo):
-    widths, cores, off, chips, members, quarters = plan(T, topo)
+    cores = list(T.cores)
     ch = topo.chip(core)
-    if ch not in chips:
+    if ch not in [topo.chip(c) for c in cores]:
         return
-    other = [o for o in chips if o != ch][0]
+    off, tab = plan(T.tables["WIDTHS"], cores, topo)
+    here = tab[ch]
+    there = tab[here["other"]]
     rank = T.rank_of(core)
     gat = T.gat
     sem = T.sem
-    sent = [0]
+    left = {"fs": 0, "snt": 0}
 
-    def one(dst, lo, hi, rsem):
-        rid, pid, _se = topo.addr(dst)
-        m = topo.mask(core, dst)
-        g.remote_dma(gat[:, lo:hi], gat[:, lo:hi], rsem, sem.snt, pid, rid, m)
-        sent[0] += bin(m).count("1")
+    def send(p, groups, rsem, lsem):
+        ap = gat[:, p["lo"]:p["hi"]]
+        trs = []
+        for m, dsts in groups:
+            ids = [DstId(rid=topo.addr(d)[0], pnc=topo.addr(d)[1]) for d in dsts]
+            trs.append(RemoteDMATransfer(dst_ids=ids, dma_engine_mask=m, remote_sem=rsem,
+                                         srcs=[ap], dsts=[ap for _d in dsts], alu_op=0))
+            left[lsem] += bin(m).count("1")
+        g.remote_dma_fused(trs, local_sem=sem[lsem])
 
-    def many(dsts, lo, hi, rsem):
-        ids = []
-        for d in dsts:
-            rid, pid, _se = topo.addr(d)
-            ids.append(DstId(rid=rid, pnc=pid))
-        g.remote_dma_fused([RemoteDMATransfer(dst_ids=ids, dma_engine_mask=0xFFFF, remote_sem=rsem,
-                                              srcs=[gat[:, lo:hi]], dsts=[gat[:, lo:hi] for _d in dsts], alu_op=0)],
-                           local_sem=sem.snt)
-        sent[0] += 16
-
-    mine = [k for k, (gc, lo, hi) in enumerate(quarters[ch]) if gc == core]
+    def cross(p, lsem):
+        send(p, [(LOW, [p["land"]])], sem["xc%d" % p["slot"]], lsem)
 
     if rank is None:
-        if not mine:
-            return
-        k = mine[0]
-        _gc, lo, hi = quarters[ch][k]
-        n = sum(1 for r in members[ch] if max(lo, off[r]) < min(hi, off[r + 1]))
-        g.wait_ge(sem.hp, 16 * n)
-        one(cores[members[other][k]], lo, hi, sem.xc)
-        g.wait_ge(sem.snt, sent[0])
+        mine = sorted([p for p in here["pieces"] if p["dist"] == core], key=lambda p: p["slot"])
+        if core in here["hg"]:
+            for p in mine:
+                g.wait_ge(sem["fd%d" % p["slot"]], p["fd_n"])
+                cross(p, "snt")
+            for p in mine:
+                send(p, [(LOW, p["to"][:1]), (HIGH, p["to"][1:])], sem["ag%d" % p["idx"]], "snt")
+        else:
+            for p in mine:
+                g.wait_ge(sem["fd%d" % p["slot"]], p["fd_n"])
+                send(p, [(ALL, p["to"])], sem["ag%d" % p["idx"]], "snt")
+        for p in sorted([p for p in there["pieces"] if p["land"] == core], key=lambda p: p["slot"]):
+            g.wait_ge(sem["xc%d" % p["slot"]], 8)
+            send(p, [(ALL, [cores[r] for r in here["mem"]])], sem["in%d" % p["idx"]], "snt")
+        g.wait_ge(sem.snt, left["snt"])
         return
 
-    w = widths[rank]
     a, b = off[rank], off[rank + 1]
-    idx = members[ch].index(rank)
-    peers = [cores[r] for r in members[ch] if r != rank]
-
-    g.sync.dma_start(gat[:, a:b], T.x[:, 0:w]).then_inc(sem.ld, 16)
-    g.scalar.dma_start(T.y[:, a:b], T.x[:, 0:w]).then_inc(sem.st_a, 16)
-    n_a = 1
-    n_s = 0
+    g.sync.dma_start(gat[:, a:b], T.x[:, 0:b - a]).then_inc(sem.ld, 16)
     g.wait_ge(sem.ld, 16)
+    feed_mask = HIGH if core in here["rg"] else ALL
+    for p in sorted([p for p in here["pieces"] if p["owner"] == rank], key=lambda p: (p["slot"], p["lo"])):
+        fd = sem["fd%d" % p["slot"]]
+        if p["gate"] == core:
+            cross(p, "fs")
+            send(p, [(feed_mask, [p["dist"]])], fd, "fs")
+        elif p["gate"] == p["dist"]:
+            send(p, [(feed_mask, [p["gate"]])], fd, "fs")
+        else:
+            send(p, [(feed_mask, [p["gate"], p["dist"]])], fd, "fs")
+    for p in here["pieces"]:
+        if p["gate"] == core and p["owner"] != rank:
+            g.wait_ge(sem["fd%d" % p["slot"]], p["fd_n"])
+            cross(p, "snt")
 
-    for gc, lo, hi in quarters[ch]:
-        if gc not in cores and max(lo, a) < min(hi, b):
-            one(gc, max(lo, a), min(hi, b), sem.hp)
-    many(peers, a, b, sem["ag%d" % idx])
-    if mine:
-        k = mine[0]
-        _gc, lo, hi = quarters[ch][k]
-        for j, r in enumerate(members[ch]):
-            if r != rank and max(lo, off[r]) < min(hi, off[r + 1]):
-                g.wait_ge(sem["ag%d" % j], 16)
-        one(cores[members[other][k]], lo, hi, sem.xc)
-    _gc, qlo, qhi = quarters[other][idx]
-    g.wait_ge(sem.xc, 8)
-    many(peers, qlo, qhi, sem["fo%d" % idx])
-
-    for j, r in enumerate(members[ch]):
-        if r != rank:
-            g.sync.wait_ge(sem["ag%d" % j], 16)
-            g.sync.dma_start(T.y[:, off[r]:off[r + 1]], gat[:, off[r]:off[r + 1]]).then_inc(sem.st_s, 16)
-            n_s += 1
-    g.scalar.wait_ge(sem.xc, 8)
-    g.scalar.dma_start(T.y[:, qlo:qhi], gat[:, qlo:qhi]).then_inc(sem.st_a, 16)
-    n_a += 1
-    for j in range(4):
-        if j != idx:
-            _gc, lo, hi = quarters[other][j]
-            g.scalar.wait_ge(sem["fo%d" % j], 16)
-            g.scalar.dma_start(T.y[:, lo:hi], gat[:, lo:hi]).then_inc(sem.st_a, 16)
-            n_a += 1
+    g.sync.wait_ge(sem.ld, 16)
+    g.sync.wait_ge(sem.fs, left["fs"])
+    g.sync.dma_start(T.y[:, a:b], gat[:, a:b]).then_inc(sem.st_s, 16)
+    n_s = 1
+    runs = []
+    for p in here["pieces"]:
+        if p["owner"] == rank:
+            continue
+        src = cores[p["owner"]] if p["gate"] == core else p["dist"]
+        if runs and runs[-1][0] == src and runs[-1][1][-1]["hi"] == p["lo"]:
+            runs[-1][1].append(p)
+        else:
+            runs.append((src, [p]))
+    runs.sort(key=lambda t: t[0] in here["hg"])
+    for _src, ps in runs:
+        for p in ps:
+            if p["gate"] == core:
+                g.sync.wait_ge(sem["fd%d" % p["slot"]], p["fd_n"])
+            else:
+                g.sync.wait_ge(sem["ag%d" % p["idx"]], p["ag_n"])
+        lo, hi = ps[0]["lo"], ps[-1]["hi"]
+        g.sync.dma_start(T.y[:, lo:hi], gat[:, lo:hi]).then_inc(sem.st_s, 16)
+        n_s += 1
+    n_a = 0
+    for p in sorted(there["pieces"], key=lambda p: (p["slot"], p["lo"])):
+        g.scalar.wait_ge(sem["in%d" % p["idx"]], 16)
+        g.scalar.dma_start(T.y[:, p["lo"]:p["hi"]], gat[:, p["lo"]:p["hi"]]).then_inc(sem.st_a, 16)
+        n_a += 1
     g.sync.wait_ge(sem.st_s, 16 * n_s)
     g.scalar.wait_ge(sem.st_a, 16 * n_a)
-    g.wait_ge(sem.snt, sent[0])
+    g.wait_ge(sem.fs, left["fs"])
+    if left["snt"]:
+        g.wait_ge(sem.snt, left["snt"])

from concourse.bass import DstId, RemoteDMATransfer

SCRATCH = {
    "gat": ("sbuf", [128, 11776], "bfloat16"),
}
SEMAPHORES = (["ld", "fs", "snt", "st_s", "st_a", "fd0", "fd1", "xc0", "xc1"]
              + ["ag%d" % i for i in range(8)] + ["in%d" % i for i in range(8)])

LOW, HIGH, ALL = 0x00FF, 0xFF00, 0xFFFF


def perms(items):
    if len(items) <= 1:
        return [list(items)]
    out = []
    for i in range(len(items)):
        for rest in perms(items[:i] + items[i + 1:]):
            out.append([items[i]] + rest)
    return out


def plan(widths, cores, topo):
    off = [0]
    for w in widths:
        off.append(off[-1] + w)
    chips = sorted(set(topo.chip(c) for c in cores))
    tab = {}
    for ch in chips:
        other = [o for o in chips if o != ch][0]
        mem = [r for r, c in enumerate(cores) if topo.chip(c) == ch]
        probe = [c for c in cores if topo.chip(c) == other][0]
        allc = list(range(ch * 8, ch * 8 + 8))
        gates = [c for c in allc if topo.may_write(c, probe)]
        hg = [c for c in gates if c not in cores]
        rg = [c for c in gates if c in cores]
        free = [c for c in allc if c not in cores and c not in gates]
        lo, hi = off[mem[0]], off[mem[-1] + 1]
        mid = (lo + hi) // 2
        cuts = [lo, (lo + mid) // 2, mid, off[cores.index(rg[1])], hi]
        pieces = []
        for k, gc in enumerate(hg + rg):
            part = []
            for r in mem:
                s, e = max(cuts[k], off[r]), min(cuts[k + 1], off[r + 1])
                if s < e:
                    part.append((s, e, r))
            if len(part) == 1:
                s, e, r = part[0]
                part = [(s, (s + e) // 2, r), ((s + e) // 2, e, r)]
            part.sort(key=lambda t: (cores[t[2]] != gc, t[0]))
            for slot, (s, e, r) in enumerate(part):
                pieces.append({"lo": s, "hi": e, "owner": r, "gate": gc, "slot": slot,
                               "dist": gc if gc in hg else free[k - 2]})
        pieces.sort(key=lambda p: p["lo"])
        for i, p in enumerate(pieces):
            p["idx"] = i
            p["to"] = [cores[r] for r in mem if r != p["owner"] and cores[r] != p["gate"]]
            p["fd_n"] = 8 if cores[p["owner"]] in rg else 16
            p["ag_n"] = 8 if p["dist"] in hg else 16
        tab[ch] = {"mem": mem, "hg": hg, "rg": rg, "free": free, "pieces": pieces, "other": other}
    for ch in chips:
        helpers = tab[ch]["hg"] + tab[ch]["free"]
        base = {h: 0 for h in helpers}
        for p in tab[ch]["pieces"]:
            n = p["hi"] - p["lo"]
            base[p["dist"]] += n * len(p["to"]) + (n if p["gate"] == p["dist"] else 0)
        inc = tab[tab[ch]["other"]]["pieces"]
        by_slot = [[p for p in inc if p["slot"] == s] for s in (0, 1)]
        best = None
        for a in perms(helpers):
            for b in perms(helpers):
                load = dict(base)
                for ps, hs in ((by_slot[0], a), (by_slot[1], b)):
                    for p, h in zip(ps, hs):
                        load[h] += 4 * (p["hi"] - p["lo"])
                m = max(load.values())
                if best is None or m < best[0]:
                    best = (m, a, b)
        for ps, hs in ((by_slot[0], best[1]), (by_slot[1], best[2])):
            for p, h in zip(ps, hs):
                p["land"] = h
    return off, tab


def rank_program(g, core, T, topo):
    cores = list(T.cores)
    ch = topo.chip(core)
    if ch not in [topo.chip(c) for c in cores]:
        return
    off, tab = plan(T.tables["WIDTHS"], cores, topo)
    here = tab[ch]
    there = tab[here["other"]]
    rank = T.rank_of(core)
    gat = T.gat
    sem = T.sem
    left = {"fs": 0, "snt": 0}

    def send(p, groups, rsem, lsem):
        ap = gat[:, p["lo"]:p["hi"]]
        trs = []
        for m, dsts in groups:
            ids = [DstId(rid=topo.addr(d)[0], pnc=topo.addr(d)[1]) for d in dsts]
            trs.append(RemoteDMATransfer(dst_ids=ids, dma_engine_mask=m, remote_sem=rsem,
                                         srcs=[ap], dsts=[ap for _d in dsts], alu_op=0))
            left[lsem] += bin(m).count("1")
        g.remote_dma_fused(trs, local_sem=sem[lsem])

    def cross(p, lsem):
        send(p, [(LOW, [p["land"]])], sem["xc%d" % p["slot"]], lsem)

    if rank is None:
        mine = sorted([p for p in here["pieces"] if p["dist"] == core], key=lambda p: p["slot"])
        if core in here["hg"]:
            for p in mine:
                g.wait_ge(sem["fd%d" % p["slot"]], p["fd_n"])
                cross(p, "snt")
            for p in mine:
                send(p, [(LOW, p["to"][:1]), (HIGH, p["to"][1:])], sem["ag%d" % p["idx"]], "snt")
        else:
            for p in mine:
                g.wait_ge(sem["fd%d" % p["slot"]], p["fd_n"])
                send(p, [(ALL, p["to"])], sem["ag%d" % p["idx"]], "snt")
        for p in sorted([p for p in there["pieces"] if p["land"] == core], key=lambda p: p["slot"]):
            g.wait_ge(sem["xc%d" % p["slot"]], 8)
            send(p, [(ALL, [cores[r] for r in here["mem"]])], sem["in%d" % p["idx"]], "snt")
        g.wait_ge(sem.snt, left["snt"])
        return

    a, b = off[rank], off[rank + 1]
    g.sync.dma_start(gat[:, a:b], T.x[:, 0:b - a]).then_inc(sem.ld, 16)
    g.wait_ge(sem.ld, 16)
    feed_mask = HIGH if core in here["rg"] else ALL
    for p in sorted([p for p in here["pieces"] if p["owner"] == rank], key=lambda p: (p["slot"], p["lo"])):
        fd = sem["fd%d" % p["slot"]]
        if p["gate"] == core:
            cross(p, "fs")
            send(p, [(feed_mask, [p["dist"]])], fd, "fs")
        elif p["gate"] == p["dist"]:
            send(p, [(feed_mask, [p["gate"]])], fd, "fs")
        else:
            send(p, [(feed_mask, [p["gate"], p["dist"]])], fd, "fs")
    for p in here["pieces"]:
        if p["gate"] == core and p["owner"] != rank:
            g.wait_ge(sem["fd%d" % p["slot"]], p["fd_n"])
            cross(p, "snt")

    g.sync.wait_ge(sem.ld, 16)
    g.sync.wait_ge(sem.fs, left["fs"])
    g.sync.dma_start(T.y[:, a:b], gat[:, a:b]).then_inc(sem.st_s, 16)
    n_s = 1
    runs = []
    for p in here["pieces"]:
        if p["owner"] == rank:
            continue
        src = cores[p["owner"]] if p["gate"] == core else p["dist"]
        if runs and runs[-1][0] == src and runs[-1][1][-1]["hi"] == p["lo"]:
            runs[-1][1].append(p)
        else:
            runs.append((src, [p]))
    runs.sort(key=lambda t: t[0] in here["hg"])
    for _src, ps in runs:
        for p in ps:
            if p["gate"] == core:
                g.sync.wait_ge(sem["fd%d" % p["slot"]], p["fd_n"])
            else:
                g.sync.wait_ge(sem["ag%d" % p["idx"]], p["ag_n"])
        lo, hi = ps[0]["lo"], ps[-1]["hi"]
        g.sync.dma_start(T.y[:, lo:hi], gat[:, lo:hi]).then_inc(sem.st_s, 16)
        n_s += 1
    n_a = 0
    for p in sorted(there["pieces"], key=lambda p: (p["slot"], p["lo"])):
        g.scalar.wait_ge(sem["in%d" % p["idx"]], 16)
        g.scalar.dma_start(T.y[:, p["lo"]:p["hi"]], gat[:, p["lo"]:p["hi"]]).then_inc(sem.st_a, 16)
        n_a += 1
    g.sync.wait_ge(sem.st_s, 16 * n_s)
    g.scalar.wait_ge(sem.st_a, 16 * n_a)
    g.wait_ge(sem.fs, left["fs"])
    if left["snt"]:
        g.wait_ge(sem.snt, left["snt"])
